import numpy as np, ml_dtypes
CORES = [21,85,149,213,277,341,405,469]
N = 8
KT, C = 4, 128
def setup_inputs(rng):
    return {"x": rng.standard_normal((N, 128, KT * C), dtype=np.float32).astype(ml_dtypes.bfloat16)}
def setup_inputs_big(rng):
    d = setup_inputs(rng)
    for k in ("x",): d[k] = (d[k].astype(np.float32) * 1024.0).astype(d[k].dtype)
    return d
def setup_inputs_small(rng):
    d = setup_inputs(rng)
    for k in ("x",): d[k] = (d[k].astype(np.float32) * (1 / 1024.0)).astype(d[k].dtype)
    return d
def setup_inputs_apart(rng):
    d = setup_inputs(rng)
    f = (10.0 ** rng.permutation(np.linspace(-1.5, 1.5, N))).astype(np.float32).reshape(N, 1, 1)
    for k in ("x",): d[k] = (d[k].astype(np.float32) * f).astype(d[k].dtype)
    return d
def reference(x):
    X = x.astype(np.float64)
    y = np.full((N, C, N * C), np.nan)
    for r in range(N):
        for i in range(N):
            s = i
            if s != r: y[r][:, C * i:C * i + C] = sum(X[r][:, C * t:C * t + C].T @ X[s][:, C * t:C * t + C] for t in range(KT))
    return {"y": y.astype(ml_dtypes.bfloat16 if x.dtype != np.float64 else np.float64)}

@@ -1,0 +1,131 @@
+from concourse.bass import DstId, RemoteDMATransfer
+
+C = 128
+KT = 4
+
+SCRATCH = {
+    "xs": ("sbuf", [128, KT * C], "bfloat16"),
+    "xq": ("sbuf", [128, KT * C], "bfloat16"),
+    "xk": ("sbuf", [128, KT * C], "bfloat16"),
+    "xp": ("sbuf", [128, KT * C], "bfloat16"),
+    "oq": ("sbuf", [128, 2 * C], "bfloat16"),
+    "ok": ("sbuf", [128, 2 * C], "bfloat16"),
+    "yo": ("sbuf", [128, 3 * C], "bfloat16"),
+    "la": ("sbuf", [128, 2 * C], "bfloat16"),
+    "lb": ("sbuf", [128, 2 * C], "bfloat16"),
+    "pa": ("psum", [128, 512], "float32"),
+    "pb": ("psum", [128, 512], "float32"),
+    "pc": ("psum", [128, 512], "float32"),
+    "pd": ("psum", [128, 512], "float32"),
+}
+SEMAPHORES = ["ld", "aq", "ak", "ap", "mma", "mmb", "mmc", "mmd", "cpa", "cpb", "cpd", "ra", "rb", "sent", "st"]
+
+
+def _plan(cores, topo):
+    def cabled(a, b):
+        return topo.rack(topo.host(a)) != topo.rack(topo.host(b)) and topo.may_write(a, b)
+
+    first = cores[0]
+    P, K, OUT = {}, {}, {}
+    for m in cores:
+        P[m] = [c for c in cores if c != m and topo.host(c) == topo.host(m)][0]
+        K[m] = [c for c in cores if cabled(m, c) and topo.chip(c) == topo.chip(m)][0]
+        straight = topo.host(m) == topo.host(first) or cabled(first, m)
+        near = [c for c in cores if topo.host(c) != topo.host(m) and topo.same_plane(c, m)]
+        OUT[m] = [c for c in near if (topo.chip(c) == topo.chip(m)) == straight][0]
+    Q = {OUT[m]: m for m in cores}
+    return P, K, OUT, Q
+
+
+def _bits(mask):
+    return [b for b in range(mask.bit_length()) if (mask >> b) & 1]
+
+
+def _mask_of(bits):
+    return sum(1 << b for b in bits)
+
+
+def rank_program(g, core, T, topo):
+    if T.rank_of(core) is None:
+        return
+    S = T.sem
+    P, K, OUT, Q = _plan(list(T.cores), topo)
+    p, k, out, q = P[core], K[core], OUT[core], Q[core]
+
+    def tile(buf, t):
+        return buf[:, t * C:(t + 1) * C]
+
+    def yblock(c):
+        return tile(T.y, T.rank_of(c))
+
+    def halves(src, dst_a, dst_b):
+        a = _bits(topo.mask(src, dst_a))[0::2]
+        b = [e for e in _bits(topo.mask(src, dst_b)) if e not in a][:len(a)]
+        return a, b
+
+    def width(src, dst):
+        return len(_bits(topo.mask(src, dst)))
+
+    g.sync.dma_start(T.xs[:], T.x[:]).then_inc(S.ld, 16)
+
+    half_out, half_k = halves(core, out, k)
+    r_out, r_k, r_p, r_q = topo.addr(out, core), topo.addr(k, core), topo.addr(p, core), topo.addr(q, core)
+    g.wait_ge(S.ld, 16)
+    g.remote_dma_fused([
+        RemoteDMATransfer(dst_ids=[DstId(rid=r_out[0], pnc=r_out[1])], dma_engine_mask=_mask_of(half_out),
+                          remote_sem=S.aq, src=T.xs[:], dst=T.xq[:]),
+        RemoteDMATransfer(dst_ids=[DstId(rid=r_k[0], pnc=r_k[1])], dma_engine_mask=_mask_of(half_k),
+                          remote_sem=S.ak, src=T.xs[:], dst=T.xk[:]),
+    ], local_sem=S.sent)
+    g.remote_dma(out_ap=T.xp[:], in_ap=T.xs[:], remote_sem=S.ap, local_sem=S.sent, pid=r_p[1], routing_id=r_p[0],
+                 dma_engine_mask=topo.mask(core, p))
+    g.wait_ge(S.cpa, 1)
+    g.remote_dma(out_ap=T.la[:], in_ap=T.oq[:], remote_sem=S.ra, local_sem=S.sent, pid=r_q[1], routing_id=r_q[0],
+                 dma_engine_mask=topo.mask(core, q))
+    g.wait_ge(S.cpb, 2)
+    g.remote_dma(out_ap=T.lb[:], in_ap=T.ok[:], remote_sem=S.rb, local_sem=S.sent, pid=r_k[1], routing_id=r_k[0],
+                 dma_engine_mask=topo.mask(core, k))
+    n_sent = len(half_out) + len(half_k) + width(core, p) + width(core, q) + width(core, k)
+
+    def gram(dst, a, b, sem):
+        for t in range(KT):
+            mm = g.tensor.matmul(dst, tile(a, t), tile(b, t), start=(t == 0), stop=(t == KT - 1))
+        mm.then_inc(sem, 1)
+
+    g.tensor.wait_ge(S.ld, 16)
+    g.tensor.wait_ge(S.aq, len(halves(q, core, K[q])[0]))
+    gram(tile(T.pa, 0), T.xq, T.xs, S.mma)
+    g.tensor.wait_ge(S.ak, len(halves(k, OUT[k], core)[1]))
+    gram(tile(T.pa, 1), T.xq, T.xk, S.mma)
+    gram(tile(T.pb, 0), T.xk, T.xq, S.mmb)
+    g.tensor.wait_ge(S.ap, width(p, core))
+    gram(tile(T.pc, 0), T.xk, T.xp, S.mmc)
+    gram(tile(T.pd, 0), T.xs, T.xq, S.mmd)
+    gram(tile(T.pd, 1), T.xs, T.xk, S.mmd)
+    gram(tile(T.pd, 2), T.xs, T.xp, S.mmd)
+
+    g.vector.wait_ge(S.mma, 2)
+    g.vector.tensor_copy(T.oq[:], T.pa[:, 0:2 * C]).then_inc(S.cpa, 1)
+    g.vector.wait_ge(S.mmb, 1)
+    g.vector.tensor_copy(tile(T.ok, 0), tile(T.pb, 0)).then_inc(S.cpb, 1)
+    g.vector.wait_ge(S.mmc, 1)
+    g.vector.tensor_copy(tile(T.ok, 1), tile(T.pc, 0)).then_inc(S.cpb, 1)
+    g.vector.wait_ge(S.mmd, 3)
+    g.vector.tensor_copy(T.yo[:], T.pd[:, 0:3 * C]).then_inc(S.cpd, 1)
+
+    n_st = 0
+    g.sync.wait_ge(S.cpd, 1)
+    g.scalar.wait_ge(S.cpd, 1)
+    g.sync.dma_start(yblock(q), tile(T.yo, 0)).then_inc(S.st, 16)
+    g.scalar.dma_start(yblock(k), tile(T.yo, 1)).then_inc(S.st, 16)
+    g.sync.dma_start(yblock(p), tile(T.yo, 2)).then_inc(S.st, 16)
+    n_st += 3
+    for sem, n, buf, who in ((S.ra, width(out, core), T.la, (out, K[out])), (S.rb, width(k, core), T.lb, (Q[k], P[k]))):
+        g.sync.wait_ge(sem, n)
+        g.scalar.wait_ge(sem, n)
+        g.sync.dma_start(yblock(who[0]), tile(buf, 0)).then_inc(S.st, 16)
+        g.scalar.dma_start(yblock(who[1]), tile(buf, 1)).then_inc(S.st, 16)
+        n_st += 2
+
+    g.wait_ge(S.sent, n_sent)
+    g.wait_ge(S.st, 16 * n_st)

@@ -9,16 +9,19 @@ SCRATCH = {
     "xk": ("sbuf", [128, KT * C], "bfloat16"),
     "xp": ("sbuf", [128, KT * C], "bfloat16"),
     "oq": ("sbuf", [128, 2 * C], "bfloat16"),
-    "ok": ("sbuf", [128, 2 * C], "bfloat16"),
+    "ok1": ("sbuf", [128, C], "bfloat16"),
+    "ok2": ("sbuf", [128, C], "bfloat16"),
     "yo": ("sbuf", [128, 3 * C], "bfloat16"),
     "la": ("sbuf", [128, 2 * C], "bfloat16"),
-    "lb": ("sbuf", [128, 2 * C], "bfloat16"),
+    "lb1": ("sbuf", [128, C], "bfloat16"),
+    "lb2": ("sbuf", [128, C], "bfloat16"),
     "pa": ("psum", [128, 512], "float32"),
     "pb": ("psum", [128, 512], "float32"),
     "pc": ("psum", [128, 512], "float32"),
     "pd": ("psum", [128, 512], "float32"),
 }
-SEMAPHORES = ["ld", "aq", "ak", "ap", "mma", "mmb", "mmc", "mmd", "cpa", "cpb", "cpd", "ra", "rb", "sent", "st"]
+SEMAPHORES = ["ld", "aq", "ak", "ap", "mma", "mmb", "mmc", "mmd", "cpa", "cpb", "cpc", "cpd", "ra", "rb1", "rb2", "sent",
+              "st"]
 
 
 def _plan(cores, topo):
@@ -66,26 +69,33 @@ def rank_program(g, core, T, topo):
     def width(src, dst):
         return len(_bits(topo.mask(src, dst)))
 
+    def xfer(dst, bits, sem, src_ap, dst_ap):
+        rid, pid = topo.addr(dst, core)
+        return RemoteDMATransfer(dst_ids=[DstId(rid=rid, pnc=pid)], dma_engine_mask=_mask_of(bits), remote_sem=sem,
+                                 src=src_ap, dst=dst_ap)
+
+    n_sent = [0]
+
+    def send(dst, sem, src_ap, dst_ap):
+        rid, pid = topo.addr(dst, core)
+        g.remote_dma(out_ap=dst_ap, in_ap=src_ap, remote_sem=sem, local_sem=S.sent, pid=pid, routing_id=rid,
+                     dma_engine_mask=topo.mask(core, dst))
+        n_sent[0] += width(core, dst)
+
     g.sync.dma_start(T.xs[:], T.x[:]).then_inc(S.ld, 16)
 
     half_out, half_k = halves(core, out, k)
-    r_out, r_k, r_p, r_q = topo.addr(out, core), topo.addr(k, core), topo.addr(p, core), topo.addr(q, core)
     g.wait_ge(S.ld, 16)
-    g.remote_dma_fused([
-        RemoteDMATransfer(dst_ids=[DstId(rid=r_out[0], pnc=r_out[1])], dma_engine_mask=_mask_of(half_out),
-                          remote_sem=S.aq, src=T.xs[:], dst=T.xq[:]),
-        RemoteDMATransfer(dst_ids=[DstId(rid=r_k[0], pnc=r_k[1])], dma_engine_mask=_mask_of(half_k),
-                          remote_sem=S.ak, src=T.xs[:], dst=T.xk[:]),
-    ], local_sem=S.sent)
-    g.remote_dma(out_ap=T.xp[:], in_ap=T.xs[:], remote_sem=S.ap, local_sem=S.sent, pid=r_p[1], routing_id=r_p[0],
-                 dma_engine_mask=topo.mask(core, p))
+    g.remote_dma_fused([xfer(out, half_out, S.aq, T.xs[:], T.xq[:]), xfer(k, half_k, S.ak, T.xs[:], T.xk[:])],
+                       local_sem=S.sent)
+    n_sent[0] += len(half_out) + len(half_k)
+    send(p, S.ap, T.xs[:], T.xp[:])
+    g.wait_ge(S.cpb, 1)
+    send(k, S.rb1, T.ok1[:], T.lb1[:])
     g.wait_ge(S.cpa, 1)
-    g.remote_dma(out_ap=T.la[:], in_ap=T.oq[:], remote_sem=S.ra, local_sem=S.sent, pid=r_q[1], routing_id=r_q[0],
-                 dma_engine_mask=topo.mask(core, q))
-    g.wait_ge(S.cpb, 2)
-    g.remote_dma(out_ap=T.lb[:], in_ap=T.ok[:], remote_sem=S.rb, local_sem=S.sent, pid=r_k[1], routing_id=r_k[0],
-                 dma_engine_mask=topo.mask(core, k))
-    n_sent = len(half_out) + len(half_k) + width(core, p) + width(core, q) + width(core, k)
+    send(q, S.ra, T.oq[:], T.la[:])
+    g.wait_ge(S.cpc, 1)
+    send(k, S.rb2, T.ok2[:], T.lb2[:])
 
     def gram(dst, a, b, sem):
         for t in range(KT):
@@ -94,38 +104,36 @@ def rank_program(g, core, T, topo):
 
     g.tensor.wait_ge(S.ld, 16)
     g.tensor.wait_ge(S.aq, len(halves(q, core, K[q])[0]))
-    gram(tile(T.pa, 0), T.xq, T.xs, S.mma)
     g.tensor.wait_ge(S.ak, len(halves(k, OUT[k], core)[1]))
-    gram(tile(T.pa, 1), T.xq, T.xk, S.mma)
     gram(tile(T.pb, 0), T.xk, T.xq, S.mmb)
+    gram(tile(T.pa, 0), T.xq, T.xs, S.mma)
+    gram(tile(T.pa, 1), T.xq, T.xk, S.mma)
     g.tensor.wait_ge(S.ap, width(p, core))
     gram(tile(T.pc, 0), T.xk, T.xp, S.mmc)
     gram(tile(T.pd, 0), T.xs, T.xq, S.mmd)
     gram(tile(T.pd, 1), T.xs, T.xk, S.mmd)
     gram(tile(T.pd, 2), T.xs, T.xp, S.mmd)
 
+    g.vector.wait_ge(S.mmb, 1)
+    g.vector.tensor_copy(T.ok1[:], tile(T.pb, 0)).then_inc(S.cpb, 1)
     g.vector.wait_ge(S.mma, 2)
     g.vector.tensor_copy(T.oq[:], T.pa[:, 0:2 * C]).then_inc(S.cpa, 1)
-    g.vector.wait_ge(S.mmb, 1)
-    g.vector.tensor_copy(tile(T.ok, 0), tile(T.pb, 0)).then_inc(S.cpb, 1)
     g.vector.wait_ge(S.mmc, 1)
-    g.vector.tensor_copy(tile(T.ok, 1), tile(T.pc, 0)).then_inc(S.cpb, 1)
+    g.vector.tensor_copy(T.ok2[:], tile(T.pc, 0)).then_inc(S.cpc, 1)
     g.vector.wait_ge(S.mmd, 3)
     g.vector.tensor_copy(T.yo[:], T.pd[:, 0:3 * C]).then_inc(S.cpd, 1)
 
-    n_st = 0
-    g.sync.wait_ge(S.cpd, 1)
+    g.sync.wait_ge(S.rb1, width(k, core))
+    g.sync.dma_start(yblock(Q[k]), T.lb1[:]).then_inc(S.st, 16)
+    g.sync.wait_ge(S.ra, width(out, core))
+    g.sync.dma_start(yblock(out), tile(T.la, 0)).then_inc(S.st, 16)
+    g.sync.dma_start(yblock(K[out]), tile(T.la, 1)).then_inc(S.st, 16)
     g.scalar.wait_ge(S.cpd, 1)
-    g.sync.dma_start(yblock(q), tile(T.yo, 0)).then_inc(S.st, 16)
+    g.scalar.dma_start(yblock(q), tile(T.yo, 0)).then_inc(S.st, 16)
     g.scalar.dma_start(yblock(k), tile(T.yo, 1)).then_inc(S.st, 16)
-    g.sync.dma_start(yblock(p), tile(T.yo, 2)).then_inc(S.st, 16)
-    n_st += 3
-    for sem, n, buf, who in ((S.ra, width(out, core), T.la, (out, K[out])), (S.rb, width(k, core), T.lb, (Q[k], P[k]))):
-        g.sync.wait_ge(sem, n)
-        g.scalar.wait_ge(sem, n)
-        g.sync.dma_start(yblock(who[0]), tile(buf, 0)).then_inc(S.st, 16)
-        g.scalar.dma_start(yblock(who[1]), tile(buf, 1)).then_inc(S.st, 16)
-        n_st += 2
+    g.scalar.dma_start(yblock(p), tile(T.yo, 2)).then_inc(S.st, 16)
+    g.scalar.wait_ge(S.rb2, width(k, core))
+    g.scalar.dma_start(yblock(P[k]), T.lb2[:]).then_inc(S.st, 16)
 
-    g.wait_ge(S.sent, n_sent)
-    g.wait_ge(S.st, 16 * n_st)
+    g.wait_ge(S.sent, n_sent[0])
+    g.wait_ge(S.st, 16 * 7)

@@ -2,26 +2,33 @@ from concourse.bass import DstId, RemoteDMATransfer
 
 C = 128
 KT = 4
+WORLD = 512
 
 SCRATCH = {
     "xs": ("sbuf", [128, KT * C], "bfloat16"),
+    "xh": ("sbuf", [128, KT * C], "bfloat16"),
     "xq": ("sbuf", [128, KT * C], "bfloat16"),
     "xk": ("sbuf", [128, KT * C], "bfloat16"),
     "xp": ("sbuf", [128, KT * C], "bfloat16"),
-    "oq": ("sbuf", [128, 2 * C], "bfloat16"),
-    "ok1": ("sbuf", [128, C], "bfloat16"),
-    "ok2": ("sbuf", [128, C], "bfloat16"),
-    "yo": ("sbuf", [128, 3 * C], "bfloat16"),
-    "la": ("sbuf", [128, 2 * C], "bfloat16"),
-    "lb1": ("sbuf", [128, C], "bfloat16"),
-    "lb2": ("sbuf", [128, C], "bfloat16"),
+    "xo": ("sbuf", [128, KT * C], "bfloat16"),
+    "xx": ("sbuf", [128, KT * C], "bfloat16"),
+    "ok": ("sbuf", [128, C], "bfloat16"),
+    "oq": ("sbuf", [128, C], "bfloat16"),
+    "y1": ("sbuf", [128, 2 * C], "bfloat16"),
+    "y2": ("sbuf", [128, C], "bfloat16"),
+    "y3": ("sbuf", [128, C], "bfloat16"),
+    "y4": ("sbuf", [128, C], "bfloat16"),
+    "la": ("sbuf", [128, C], "bfloat16"),
+    "lb": ("sbuf", [128, C], "bfloat16"),
     "pa": ("psum", [128, 512], "float32"),
     "pb": ("psum", [128, 512], "float32"),
     "pc": ("psum", [128, 512], "float32"),
     "pd": ("psum", [128, 512], "float32"),
+    "pe": ("psum", [128, 512], "float32"),
+    "pf": ("psum", [128, 512], "float32"),
 }
-SEMAPHORES = ["ld", "aq", "ak", "ap", "mma", "mmb", "mmc", "mmd", "cpa", "cpb", "cpc", "cpd", "ra", "rb1", "rb2", "sent",
-              "st"]
+SEMAPHORES = ["ld", "ah", "aq", "ak", "ap", "ao", "ax", "mma", "mmb", "mmc", "mmd", "mme", "mmf",
+              "cpt", "cpc", "cpd", "cpe", "cpf", "ra", "rb", "sent", "st"]
 
 
 def _plan(cores, topo):
@@ -29,15 +36,19 @@ def _plan(cores, topo):
         return topo.rack(topo.host(a)) != topo.rack(topo.host(b)) and topo.may_write(a, b)
 
     first = cores[0]
-    P, K, OUT = {}, {}, {}
+    P, K, OUT, H = {}, {}, {}, {}
     for m in cores:
         P[m] = [c for c in cores if c != m and topo.host(c) == topo.host(m)][0]
         K[m] = [c for c in cores if cabled(m, c) and topo.chip(c) == topo.chip(m)][0]
         straight = topo.host(m) == topo.host(first) or cabled(first, m)
         near = [c for c in cores if topo.host(c) != topo.host(m) and topo.same_plane(c, m)]
         OUT[m] = [c for c in near if (topo.chip(c) == topo.chip(m)) == straight][0]
+        far = [c for c in range(WORLD) if c not in cores and topo.host(c) == topo.host(m)
+               and topo.chip(c) == topo.chip(m) and topo.die(c) != topo.die(m)]
+        H[m] = [far[0], far[-1]]
     Q = {OUT[m]: m for m in cores}
-    return P, K, OUT, Q
+    X = {m: P[K[m]] for m in cores}
+    return P, K, OUT, Q, X, H
 
 
 def _bits(mask):
@@ -49,22 +60,23 @@ def _mask_of(bits):
 
 
 def rank_program(g, core, T, topo):
-    if T.rank_of(core) is None:
-        return
     S = T.sem
-    P, K, OUT, Q = _plan(list(T.cores), topo)
-    p, k, out, q = P[core], K[core], OUT[core], Q[core]
-
-    def tile(buf, t):
-        return buf[:, t * C:(t + 1) * C]
-
-    def yblock(c):
-        return tile(T.y, T.rank_of(c))
+    P, K, OUT, Q, X, H = _plan(list(T.cores), topo)
+    served = {H[m][j]: (m, j) for m in H for j in range(len(H[m]))}
+    if T.rank_of(core) is None and core not in served:
+        return
 
     def halves(src, dst_a, dst_b):
         a = _bits(topo.mask(src, dst_a))[0::2]
         b = [e for e in _bits(topo.mask(src, dst_b)) if e not in a][:len(a)]
         return a, b
+
+    def inner(m, j):
+        return [e for e in _bits(topo.mask(m, H[m][j])) if e not in _bits(topo.mask(m, OUT[m]))][j::len(H[m])]
+
+    def part(buf, j):
+        w = KT * C // 2
+        return buf[:, j * w:(j + 1) * w]
 
     def width(src, dst):
         return len(_bits(topo.mask(src, dst)))
@@ -74,13 +86,30 @@ def rank_program(g, core, T, topo):
         return RemoteDMATransfer(dst_ids=[DstId(rid=rid, pnc=pid)], dma_engine_mask=_mask_of(bits), remote_sem=sem,
                                  src=src_ap, dst=dst_ap)
 
+    if core in served:
+        m, j = served[core]
+        a, b = halves(core, Q[m], X[m])
+        g.wait_ge(S.ah, len(inner(m, j)))
+        g.remote_dma_fused([xfer(Q[m], a, S.ao, part(T.xh, j), part(T.xo, j)),
+                            xfer(X[m], b, S.ax, part(T.xh, j), part(T.xx, j))], local_sem=S.sent)
+        g.wait_ge(S.sent, len(a) + len(b))
+        return
+
+    p, k, out, q, x, h = P[core], K[core], OUT[core], Q[core], X[core], H[core]
+
+    def tile(buf, t):
+        return buf[:, t * C:(t + 1) * C]
+
+    def yblock(c):
+        return tile(T.y, T.rank_of(c))
+
     n_sent = [0]
 
-    def send(dst, sem, src_ap, dst_ap):
+    def send(dst, bits, sem, src_ap, dst_ap):
         rid, pid = topo.addr(dst, core)
         g.remote_dma(out_ap=dst_ap, in_ap=src_ap, remote_sem=sem, local_sem=S.sent, pid=pid, routing_id=rid,
-                     dma_engine_mask=topo.mask(core, dst))
-        n_sent[0] += width(core, dst)
+                     dma_engine_mask=_mask_of(bits))
+        n_sent[0] += len(bits)
 
     g.sync.dma_start(T.xs[:], T.x[:]).then_inc(S.ld, 16)
 
@@ -89,13 +118,15 @@ def rank_program(g, core, T, topo):
     g.remote_dma_fused([xfer(out, half_out, S.aq, T.xs[:], T.xq[:]), xfer(k, half_k, S.ak, T.xs[:], T.xk[:])],
                        local_sem=S.sent)
     n_sent[0] += len(half_out) + len(half_k)
-    send(p, S.ap, T.xs[:], T.xp[:])
-    g.wait_ge(S.cpb, 1)
-    send(k, S.rb1, T.ok1[:], T.lb1[:])
-    g.wait_ge(S.cpa, 1)
-    send(q, S.ra, T.oq[:], T.la[:])
-    g.wait_ge(S.cpc, 1)
-    send(k, S.rb2, T.ok2[:], T.lb2[:])
+    g.remote_dma_fused([xfer(h[j], inner(core, j), S.ah, part(T.xs, j), part(T.xh, j)) for j in range(len(h))],
+                       local_sem=S.sent)
+    n_sent[0] += sum(len(inner(core, j)) for j in range(len(h)))
+    send(p, _bits(topo.mask(core, p)), S.ap, T.xs[:], T.xp[:])
+    half_q, half_k2 = halves(core, q, k)
+    g.wait_ge(S.cpt, 2)
+    g.remote_dma_fused([xfer(q, half_q, S.ra, T.oq[:], T.la[:]), xfer(k, half_k2, S.rb, T.ok[:], T.lb[:])],
+                       local_sem=S.sent)
+    n_sent[0] += len(half_q) + len(half_k2)
 
     def gram(dst, a, b, sem):
         for t in range(KT):
@@ -105,35 +136,43 @@ def rank_program(g, core, T, topo):
     g.tensor.wait_ge(S.ld, 16)
     g.tensor.wait_ge(S.aq, len(halves(q, core, K[q])[0]))
     g.tensor.wait_ge(S.ak, len(halves(k, OUT[k], core)[1]))
-    gram(tile(T.pb, 0), T.xk, T.xq, S.mmb)
-    gram(tile(T.pa, 0), T.xq, T.xs, S.mma)
-    gram(tile(T.pa, 1), T.xq, T.xk, S.mma)
+    gram(tile(T.pa, 0), T.xk, T.xq, S.mma)
+    gram(tile(T.pb, 0), T.xq, T.xk, S.mmb)
+    gram(tile(T.pc, 0), T.xs, T.xq, S.mmc)
+    gram(tile(T.pc, 1), T.xs, T.xk, S.mmc)
     g.tensor.wait_ge(S.ap, width(p, core))
-    gram(tile(T.pc, 0), T.xk, T.xp, S.mmc)
-    gram(tile(T.pd, 0), T.xs, T.xq, S.mmd)
-    gram(tile(T.pd, 1), T.xs, T.xk, S.mmd)
-    gram(tile(T.pd, 2), T.xs, T.xp, S.mmd)
+    gram(tile(T.pd, 0), T.xs, T.xp, S.mmd)
+    g.tensor.wait_ge(S.ao, sum(len(halves(c, core, X[out])[0]) for c in H[out]))
+    gram(tile(T.pe, 0), T.xs, T.xo, S.mme)
+    g.tensor.wait_ge(S.ax, sum(len(halves(c, Q[x], core)[1]) for c in H[x]))
+    gram(tile(T.pf, 0), T.xs, T.xx, S.mmf)
 
+    g.vector.wait_ge(S.mma, 1)
+    g.vector.tensor_copy(T.ok[:], tile(T.pa, 0)).then_inc(S.cpt, 1)
     g.vector.wait_ge(S.mmb, 1)
-    g.vector.tensor_copy(T.ok1[:], tile(T.pb, 0)).then_inc(S.cpb, 1)
-    g.vector.wait_ge(S.mma, 2)
-    g.vector.tensor_copy(T.oq[:], T.pa[:, 0:2 * C]).then_inc(S.cpa, 1)
-    g.vector.wait_ge(S.mmc, 1)
-    g.vector.tensor_copy(T.ok2[:], tile(T.pc, 0)).then_inc(S.cpc, 1)
-    g.vector.wait_ge(S.mmd, 3)
-    g.vector.tensor_copy(T.yo[:], T.pd[:, 0:3 * C]).then_inc(S.cpd, 1)
+    g.vector.tensor_copy(T.oq[:], tile(T.pb, 0)).then_inc(S.cpt, 1)
+    g.vector.wait_ge(S.mmc, 2)
+    g.vector.tensor_copy(T.y1[:], T.pc[:, 0:2 * C]).then_inc(S.cpc, 1)
+    g.vector.wait_ge(S.mmd, 1)
+    g.vector.tensor_copy(T.y2[:], tile(T.pd, 0)).then_inc(S.cpd, 1)
+    g.vector.wait_ge(S.mme, 1)
+    g.vector.tensor_copy(T.y3[:], tile(T.pe, 0)).then_inc(S.cpe, 1)
+    g.vector.wait_ge(S.mmf, 1)
+    g.vector.tensor_copy(T.y4[:], tile(T.pf, 0)).then_inc(S.cpf, 1)
 
-    g.sync.wait_ge(S.rb1, width(k, core))
-    g.sync.dma_start(yblock(Q[k]), T.lb1[:]).then_inc(S.st, 16)
-    g.sync.wait_ge(S.ra, width(out, core))
-    g.sync.dma_start(yblock(out), tile(T.la, 0)).then_inc(S.st, 16)
-    g.sync.dma_start(yblock(K[out]), tile(T.la, 1)).then_inc(S.st, 16)
+    g.sync.wait_ge(S.cpc, 1)
+    g.sync.dma_start(yblock(q), tile(T.y1, 0)).then_inc(S.st, 16)
+    g.sync.dma_start(yblock(k), tile(T.y1, 1)).then_inc(S.st, 16)
+    g.sync.wait_ge(S.rb, len(halves(k, Q[k], core)[1]))
+    g.sync.dma_start(yblock(Q[k]), T.lb[:]).then_inc(S.st, 16)
+    g.sync.wait_ge(S.ra, len(halves(out, core, K[out])[0]))
+    g.sync.dma_start(yblock(K[out]), T.la[:]).then_inc(S.st, 16)
     g.scalar.wait_ge(S.cpd, 1)
-    g.scalar.dma_start(yblock(q), tile(T.yo, 0)).then_inc(S.st, 16)
-    g.scalar.dma_start(yblock(k), tile(T.yo, 1)).then_inc(S.st, 16)
-    g.scalar.dma_start(yblock(p), tile(T.yo, 2)).then_inc(S.st, 16)
-    g.scalar.wait_ge(S.rb2, width(k, core))
-    g.scalar.dma_start(yblock(P[k]), T.lb2[:]).then_inc(S.st, 16)
+    g.scalar.dma_start(yblock(p), T.y2[:]).then_inc(S.st, 16)
+    g.scalar.wait_ge(S.cpe, 1)
+    g.scalar.dma_start(yblock(out), T.y3[:]).then_inc(S.st, 16)
+    g.scalar.wait_ge(S.cpf, 1)
+    g.scalar.dma_start(yblock(x), T.y4[:]).then_inc(S.st, 16)
 
     g.wait_ge(S.sent, n_sent[0])
     g.wait_ge(S.st, 16 * 7)

from concourse.bass import DstId, RemoteDMATransfer

C = 128
KT = 4
WORLD = 512

SCRATCH = {
    "xs": ("sbuf", [128, KT * C], "bfloat16"),
    "xh": ("sbuf", [128, KT * C], "bfloat16"),
    "xq": ("sbuf", [128, KT * C], "bfloat16"),
    "xk": ("sbuf", [128, KT * C], "bfloat16"),
    "xp": ("sbuf", [128, KT * C], "bfloat16"),
    "xo": ("sbuf", [128, KT * C], "bfloat16"),
    "xx": ("sbuf", [128, KT * C], "bfloat16"),
    "ok": ("sbuf", [128, C], "bfloat16"),
    "oq": ("sbuf", [128, C], "bfloat16"),
    "y1": ("sbuf", [128, 2 * C], "bfloat16"),
    "y2": ("sbuf", [128, C], "bfloat16"),
    "y3": ("sbuf", [128, C], "bfloat16"),
    "y4": ("sbuf", [128, C], "bfloat16"),
    "la": ("sbuf", [128, C], "bfloat16"),
    "lb": ("sbuf", [128, C], "bfloat16"),
    "pa": ("psum", [128, 512], "float32"),
    "pb": ("psum", [128, 512], "float32"),
    "pc": ("psum", [128, 512], "float32"),
    "pd": ("psum", [128, 512], "float32"),
    "pe": ("psum", [128, 512], "float32"),
    "pf": ("psum", [128, 512], "float32"),
}
SEMAPHORES = ["ld", "ah", "aq", "ak", "ap", "ao", "ax", "mma", "mmb", "mmc", "mmd", "mme", "mmf",
              "cpt", "cpc", "cpd", "cpe", "cpf", "ra", "rb", "sent", "st"]


def _plan(cores, topo):
    def cabled(a, b):
        return topo.rack(topo.host(a)) != topo.rack(topo.host(b)) and topo.may_write(a, b)

    first = cores[0]
    P, K, OUT, H = {}, {}, {}, {}
    for m in cores:
        P[m] = [c for c in cores if c != m and topo.host(c) == topo.host(m)][0]
        K[m] = [c for c in cores if cabled(m, c) and topo.chip(c) == topo.chip(m)][0]
        straight = topo.host(m) == topo.host(first) or cabled(first, m)
        near = [c for c in cores if topo.host(c) != topo.host(m) and topo.same_plane(c, m)]
        OUT[m] = [c for c in near if (topo.chip(c) == topo.chip(m)) == straight][0]
        far = [c for c in range(WORLD) if c not in cores and topo.host(c) == topo.host(m)
               and topo.chip(c) == topo.chip(m) and topo.die(c) != topo.die(m)]
        H[m] = [far[0], far[-1]]
    Q = {OUT[m]: m for m in cores}
    X = {m: P[K[m]] for m in cores}
    return P, K, OUT, Q, X, H


def _bits(mask):
    return [b for b in range(mask.bit_length()) if (mask >> b) & 1]


def _mask_of(bits):
    return sum(1 << b for b in bits)


def rank_program(g, core, T, topo):
    S = T.sem
    P, K, OUT, Q, X, H = _plan(list(T.cores), topo)
    served = {H[m][j]: (m, j) for m in H for j in range(len(H[m]))}
    if T.rank_of(core) is None and core not in served:
        return

    def halves(src, dst_a, dst_b):
        a = _bits(topo.mask(src, dst_a))[0::2]
        b = [e for e in _bits(topo.mask(src, dst_b)) if e not in a][:len(a)]
        return a, b

    def inner(m, j):
        return [e for e in _bits(topo.mask(m, H[m][j])) if e not in _bits(topo.mask(m, OUT[m]))][j::len(H[m])]

    def part(buf, j):
        w = KT * C // 2
        return buf[:, j * w:(j + 1) * w]

    def width(src, dst):
        return len(_bits(topo.mask(src, dst)))

    def xfer(dst, bits, sem, src_ap, dst_ap):
        rid, pid = topo.addr(dst, core)
        return RemoteDMATransfer(dst_ids=[DstId(rid=rid, pnc=pid)], dma_engine_mask=_mask_of(bits), remote_sem=sem,
                                 src=src_ap, dst=dst_ap)

    if core in served:
        m, j = served[core]
        a, b = halves(core, Q[m], X[m])
        g.wait_ge(S.ah, len(inner(m, j)))
        g.remote_dma_fused([xfer(Q[m], a, S.ao, part(T.xh, j), part(T.xo, j)),
                            xfer(X[m], b, S.ax, part(T.xh, j), part(T.xx, j))], local_sem=S.sent)
        g.wait_ge(S.sent, len(a) + len(b))
        return

    p, k, out, q, x, h = P[core], K[core], OUT[core], Q[core], X[core], H[core]

    def tile(buf, t):
        return buf[:, t * C:(t + 1) * C]

    def yblock(c):
        return tile(T.y, T.rank_of(c))

    n_sent = [0]

    def send(dst, bits, sem, src_ap, dst_ap):
        rid, pid = topo.addr(dst, core)
        g.remote_dma(out_ap=dst_ap, in_ap=src_ap, remote_sem=sem, local_sem=S.sent, pid=pid, routing_id=rid,
                     dma_engine_mask=_mask_of(bits))
        n_sent[0] += len(bits)

    g.sync.dma_start(T.xs[:], T.x[:]).then_inc(S.ld, 16)

    half_out, half_k = halves(core, out, k)
    g.wait_ge(S.ld, 16)
    g.remote_dma_fused([xfer(out, half_out, S.aq, T.xs[:], T.xq[:]), xfer(k, half_k, S.ak, T.xs[:], T.xk[:])],
                       local_sem=S.sent)
    n_sent[0] += len(half_out) + len(half_k)
    g.remote_dma_fused([xfer(h[j], inner(core, j), S.ah, part(T.xs, j), part(T.xh, j)) for j in range(len(h))],
                       local_sem=S.sent)
    n_sent[0] += sum(len(inner(core, j)) for j in range(len(h)))
    send(p, _bits(topo.mask(core, p)), S.ap, T.xs[:], T.xp[:])
    half_q, half_k2 = halves(core, q, k)
    g.wait_ge(S.cpt, 2)
    g.remote_dma_fused([xfer(q, half_q, S.ra, T.oq[:], T.la[:]), xfer(k, half_k2, S.rb, T.ok[:], T.lb[:])],
                       local_sem=S.sent)
    n_sent[0] += len(half_q) + len(half_k2)

    def gram(dst, a, b, sem):
        for t in range(KT):
            mm = g.tensor.matmul(dst, tile(a, t), tile(b, t), start=(t == 0), stop=(t == KT - 1))
        mm.then_inc(sem, 1)

    g.tensor.wait_ge(S.ld, 16)
    g.tensor.wait_ge(S.aq, len(halves(q, core, K[q])[0]))
    g.tensor.wait_ge(S.ak, len(halves(k, OUT[k], core)[1]))
    gram(tile(T.pa, 0), T.xk, T.xq, S.mma)
    gram(tile(T.pb, 0), T.xq, T.xk, S.mmb)
    gram(tile(T.pc, 0), T.xs, T.xq, S.mmc)
    gram(tile(T.pc, 1), T.xs, T.xk, S.mmc)
    g.tensor.wait_ge(S.ap, width(p, core))
    gram(tile(T.pd, 0), T.xs, T.xp, S.mmd)
    g.tensor.wait_ge(S.ao, sum(len(halves(c, core, X[out])[0]) for c in H[out]))
    gram(tile(T.pe, 0), T.xs, T.xo, S.mme)
    g.tensor.wait_ge(S.ax, sum(len(halves(c, Q[x], core)[1]) for c in H[x]))
    gram(tile(T.pf, 0), T.xs, T.xx, S.mmf)

    g.vector.wait_ge(S.mma, 1)
    g.vector.tensor_copy(T.ok[:], tile(T.pa, 0)).then_inc(S.cpt, 1)
    g.vector.wait_ge(S.mmb, 1)
    g.vector.tensor_copy(T.oq[:], tile(T.pb, 0)).then_inc(S.cpt, 1)
    g.vector.wait_ge(S.mmc, 2)
    g.vector.tensor_copy(T.y1[:], T.pc[:, 0:2 * C]).then_inc(S.cpc, 1)
    g.vector.wait_ge(S.mmd, 1)
    g.vector.tensor_copy(T.y2[:], tile(T.pd, 0)).then_inc(S.cpd, 1)
    g.vector.wait_ge(S.mme, 1)
    g.vector.tensor_copy(T.y3[:], tile(T.pe, 0)).then_inc(S.cpe, 1)
    g.vector.wait_ge(S.mmf, 1)
    g.vector.tensor_copy(T.y4[:], tile(T.pf, 0)).then_inc(S.cpf, 1)

    g.sync.wait_ge(S.cpc, 1)
    g.sync.dma_start(yblock(q), tile(T.y1, 0)).then_inc(S.st, 16)
    g.sync.dma_start(yblock(k), tile(T.y1, 1)).then_inc(S.st, 16)
    g.sync.wait_ge(S.rb, len(halves(k, Q[k], core)[1]))
    g.sync.dma_start(yblock(Q[k]), T.lb[:]).then_inc(S.st, 16)
    g.sync.wait_ge(S.ra, len(halves(out, core, K[out])[0]))
    g.sync.dma_start(yblock(K[out]), T.la[:]).then_inc(S.st, 16)
    g.scalar.wait_ge(S.cpd, 1)
    g.scalar.dma_start(yblock(p), T.y2[:]).then_inc(S.st, 16)
    g.scalar.wait_ge(S.cpe, 1)
    g.scalar.dma_start(yblock(out), T.y3[:]).then_inc(S.st, 16)
    g.scalar.wait_ge(S.cpf, 1)
    g.scalar.dma_start(yblock(x), T.y4[:]).then_inc(S.st, 16)

    g.wait_ge(S.sent, n_sent[0])
    g.wait_ge(S.st, 16 * 7)
